import numpy as np
import ml_dtypes


def mxq(x, axis, fmt="e4m3"):
    dtype, down = {"e4m3": (ml_dtypes.float8_e4m3fn, 7), "e5m2": (ml_dtypes.float8_e5m2, 14)}[fmt]
    v = np.moveaxis(np.asarray(x, np.float32).astype(ml_dtypes.bfloat16).astype(np.float64), axis, -1)
    blocks = v.reshape(v.shape[:-1] + (-1, 32))
    amax = np.abs(blocks).max(-1, keepdims=True)
    byte = np.maximum(np.where(amax > 0, np.frexp(amax)[1] - 1 + 127, 0) - down, 1)
    scale = np.exp2(byte - 127.0)
    codes = (blocks / scale).astype(np.float32).astype(dtype).astype(np.float64)
    return np.moveaxis((codes * scale).reshape(v.shape), -1, axis)


WIDE = False


def mx_kscale(k):
    if not WIDE:
        return np.ones(k)
    levels = np.array([10, -10, 5, -5, 0])
    if k % 512:
        return np.exp2(np.random.permutation(np.resize(levels, k // 32))).repeat(32)
    a = np.empty((k // 512, 16))
    for p in range(k // 512):
        a[p, :8] = np.random.permutation(np.resize(levels, 8))
        for g in range(8):
            far = levels[np.abs(levels - a[p, g]) >= 10]
            a[p, g + 8] = far[np.random.randint(len(far))]
    return np.exp2(a.ravel()).repeat(32)


def f64(x):
    return np.asarray(x).astype(np.float64)


def striped8(idx):
    return np.concatenate([v.reshape(-1, 16).T for v in idx]).astype(np.uint16)


def unstriped8(offs):
    return np.stack([offs[16 * g:16 * g + 16].T.reshape(-1) for g in range(8)]).astype(np.int64)


K, M, T, S = 1024, 512, 512, 256


def setup_inputs():
    n = np.random.standard_normal
    s = mx_kscale(K)[:, None]
    return {
        "x": (n((K, S)) * s).astype(np.float32),
        "w": (n((K, M)) / np.sqrt(K) / s).astype(np.float32),
        "wgo": np.repeat(np.random.uniform(0.5, 2.0, (8, S)), 16, axis=0).astype(np.float32),
        "offs": striped8(np.stack([np.random.permutation(T)[:S] for _ in range(8)])),
    }


def reference(x, w, wgo, offs):
    x_ = mxq(f64(x), 0, "e4m3")
    w_ = mxq(f64(w), 0, "e4m3")
    y = w_.T @ x_
    place = unstriped8(offs)[np.arange(M) % 128 // 16]
    out = np.zeros((M, T))
    out[np.arange(M)[:, None], place] = f64(wgo)[np.arange(M) % 128] * (y)
    return out

@@ -1,0 +1,129 @@
+from contextlib import ExitStack
+
+import concourse.mybir as mybir
+
+K, M, T, S = 1024, 512, 512, 256
+FLOPS = 2 * K * M * S
+
+F32 = mybir.dt.float32
+BF16 = mybir.dt.bfloat16
+U32 = mybir.dt.uint32
+U16 = mybir.dt.uint16
+U8 = mybir.dt.uint8
+FP8X4 = mybir.dt.float8_e4m3fn_x4
+MULT = mybir.AluOpType.mult
+
+P = 128
+PACK = 4
+K_PASS = P * PACK
+PASSES = K // K_PASS
+BLOCKS = M // P
+HALF = S // 2
+HALVES = S // HALF
+LIST_COLS = HALF // 16
+X_SPLIT = 96
+W_SPLIT = 64
+
+
+def tile_list_hscat_none_kernel(tc, x, w, wgo, offs, out):
+    nc = tc.nc
+    with ExitStack() as ctx:
+        keep = ctx.enter_context(tc.tile_pool(name="keep", bufs=1))
+        psum = ctx.enter_context(tc.psum_pool(name="psum", bufs=1))
+
+        offsets = keep.tile([P, S // 16], U16, name="offsets")
+        weights = keep.tile([P, S], F32, name="weights")
+        x_raw = [keep.tile([P, PACK, S], F32, name=f"x_raw{a}") for a in range(PASSES)]
+        w_raw = [[keep.tile([P, PACK, P], F32, name=f"w_raw{m}_{a}") for a in range(PASSES)] for m in range(BLOCKS)]
+        x_grouped = [keep.tile([P, S, PACK], BF16, name=f"x_grouped{a}", align_bytes=64) for a in range(PASSES)]
+        x_codes = [keep.tile([P, S], U32, name=f"x_codes{a}", align_bytes=64) for a in range(PASSES)]
+        x_scales = [keep.tile([P, S], U8, name=f"x_scales{a}", align_bytes=64) for a in range(PASSES)]
+        w_grouped = [keep.tile([P, PASSES * P, PACK], BF16, name=f"w_grouped{m}", align_bytes=64) for m in range(BLOCKS)]
+        w_codes = [keep.tile([P, PASSES * P], U32, name=f"w_codes{m}", align_bytes=64) for m in range(BLOCKS)]
+        w_scales = [keep.tile([P, PASSES * P], U8, name=f"w_scales{m}", align_bytes=64) for m in range(BLOCKS)]
+        windows = [keep.tile([P, T], F32, name=f"window{m}") for m in range(BLOCKS)]
+        y = [[keep.tile([P, HALF], F32, name=f"y{m}_{h}") for h in range(HALVES)] for m in range(BLOCKS)]
+        acc = [[psum.tile([P, HALF], F32, name=f"acc{m}_{h}") for h in range(HALVES)] for m in range(BLOCKS)]
+
+        def load_x(a):
+            nc.sync.dma_start(out=x_raw[a][:], in_=x[a * K_PASS : (a + 1) * K_PASS, :].rearrange("(p j) s -> p j s", j=PACK))
+
+        def load_w(m, a):
+            nc.sync.dma_start(
+                out=w_raw[m][a][:],
+                in_=w[a * K_PASS : (a + 1) * K_PASS, m * P : (m + 1) * P].rearrange("(p j) n -> p j n", j=PACK),
+            )
+
+        def interleave(copy, grouped, raw, c0, c1, base=0):
+            copy(out=grouped[:, base + c0 : base + c1, :], in_=raw[:, :, c0:c1].rearrange("p j c -> p c j"))
+
+        def quantise(codes, scales, grouped, c0, c1):
+            nc.vector.quantize_mx(
+                out=codes[:, c0:c1].bitcast(FP8X4),
+                scales=scales[:, c0:c1],
+                in_=grouped[:, c0:c1, :].rearrange("p c j -> p (c j)"),
+            )
+
+        def multiply(m, a):
+            for h in range(HALVES):
+                nc.tensor.matmul_mx(
+                    out=acc[m][h][:],
+                    lhsT=w_codes[m][:, a * P : (a + 1) * P].bitcast(FP8X4),
+                    lhsT_scale=w_scales[m][:, a * P : (a + 1) * P],
+                    rhs=x_codes[a][:, h * HALF : (h + 1) * HALF].bitcast(FP8X4),
+                    rhs_scale=x_scales[a][:, h * HALF : (h + 1) * HALF],
+                    start=(a == 0),
+                    stop=(a == PASSES - 1),
+                )
+
+        def empty(m):
+            for h in range(HALVES):
+                nc.scalar.copy(out=y[m][h][:], in_=acc[m][h][:])
+
+        def scatter(m, h):
+            nc.vector.tensor_tensor(
+                windows[m][:].indirect(offsets[:, h * LIST_COLS : (h + 1) * LIST_COLS]),
+                y[m][h][:],
+                weights[:, h * HALF : (h + 1) * HALF],
+                MULT,
+            )
+
+        def store(m):
+            nc.sync.dma_start(out=out[m * P : (m + 1) * P, :], in_=windows[m][:])
+
+        for a in range(PASSES):
+            load_x(a)
+            load_w(0, a)
+        nc.sync.dma_start(offsets[:], offs)
+        nc.sync.dma_start(out=weights[:], in_=wgo)
+        for m in range(1, BLOCKS):
+            for a in range(PASSES):
+                load_w(m, a)
+
+        for m in range(BLOCKS):
+            nc.gpsimd.memset(windows[m][:], 0.0)
+
+        for a in range(PASSES):
+            interleave(nc.scalar.copy, x_grouped[a], x_raw[a], 0, X_SPLIT)
+            interleave(nc.vector.tensor_copy, x_grouped[a], x_raw[a], X_SPLIT, S)
+            quantise(x_codes[a], x_scales[a], x_grouped[a], 0, S)
+            interleave(nc.scalar.copy, w_grouped[0], w_raw[0][a], 0, W_SPLIT, base=a * P)
+            interleave(nc.vector.tensor_copy, w_grouped[0], w_raw[0][a], W_SPLIT, P, base=a * P)
+            quantise(w_codes[0], w_scales[0], w_grouped[0], a * P, (a + 1) * P)
+            multiply(0, a)
+        empty(0)
+        interleave(nc.vector.tensor_copy, w_grouped[1], w_raw[1][0], 0, P)
+        interleave(nc.scalar.copy, w_grouped[1], w_raw[1][1], 0, P, base=P)
+
+        for m in range(BLOCKS):
+            scatter(m, 0)
+            if m + 1 < BLOCKS:
+                quantise(w_codes[m + 1], w_scales[m + 1], w_grouped[m + 1], 0, PASSES * P)
+                for a in range(PASSES):
+                    multiply(m + 1, a)
+                empty(m + 1)
+            if m + 2 < BLOCKS:
+                for a in range(PASSES):
+                    interleave(nc.scalar.copy, w_grouped[m + 2], w_raw[m + 2][a], 0, P, base=a * P)
+            scatter(m, 1)
+            store(m)

@@ -23,6 +23,7 @@ HALVES = S // HALF
 LIST_COLS = HALF // 16
 X_SPLIT = 96
 W_SPLIT = 64
+Y_SLOT = (1, 0, 0, 0)
 
 
 def tile_list_hscat_none_kernel(tc, x, w, wgo, offs, out):
@@ -34,7 +35,7 @@ def tile_list_hscat_none_kernel(tc, x, w, wgo, offs, out):
         offsets = keep.tile([P, S // 16], U16, name="offsets")
         weights = keep.tile([P, S], F32, name="weights")
         x_raw = [keep.tile([P, PACK, S], F32, name=f"x_raw{a}") for a in range(PASSES)]
-        w_raw = [[keep.tile([P, PACK, P], F32, name=f"w_raw{m}_{a}") for a in range(PASSES)] for m in range(BLOCKS)]
+        w_raw = [[keep.tile([P, PACK, P], F32, name=f"w_raw{m}_{a}", tag=f"slot{m}_{a}") for a in range(PASSES)] for m in range(BLOCKS)]
         x_grouped = [keep.tile([P, S, PACK], BF16, name=f"x_grouped{a}", align_bytes=64) for a in range(PASSES)]
         x_codes = [keep.tile([P, S], U32, name=f"x_codes{a}", align_bytes=64) for a in range(PASSES)]
         x_scales = [keep.tile([P, S], U8, name=f"x_scales{a}", align_bytes=64) for a in range(PASSES)]
@@ -42,8 +43,8 @@ def tile_list_hscat_none_kernel(tc, x, w, wgo, offs, out):
         w_codes = [keep.tile([P, PASSES * P], U32, name=f"w_codes{m}", align_bytes=64) for m in range(BLOCKS)]
         w_scales = [keep.tile([P, PASSES * P], U8, name=f"w_scales{m}", align_bytes=64) for m in range(BLOCKS)]
         windows = [keep.tile([P, T], F32, name=f"window{m}") for m in range(BLOCKS)]
-        y = [[keep.tile([P, HALF], F32, name=f"y{m}_{h}") for h in range(HALVES)] for m in range(BLOCKS)]
-        acc = [[psum.tile([P, HALF], F32, name=f"acc{m}_{h}") for h in range(HALVES)] for m in range(BLOCKS)]
+        acc = [[psum.tile([P, HALF], F32, name=f"acc{m}_{h}") for h in range(HALVES)] for m in range(1)] + [[psum.tile([P, S], F32, name=f"acc{m}")] for m in range(1, BLOCKS)]
+        y = {}
 
         def load_x(a):
             nc.sync.dma_start(out=x_raw[a][:], in_=x[a * K_PASS : (a + 1) * K_PASS, :].rearrange("(p j) s -> p j s", j=PACK))
@@ -65,25 +66,28 @@ def tile_list_hscat_none_kernel(tc, x, w, wgo, offs, out):
             )
 
         def multiply(m, a):
-            for h in range(HALVES):
+            for i, bank in enumerate(acc[m]):
+                n = S // len(acc[m])
                 nc.tensor.matmul_mx(
-                    out=acc[m][h][:],
+                    out=bank[:],
                     lhsT=w_codes[m][:, a * P : (a + 1) * P].bitcast(FP8X4),
                     lhsT_scale=w_scales[m][:, a * P : (a + 1) * P],
-                    rhs=x_codes[a][:, h * HALF : (h + 1) * HALF].bitcast(FP8X4),
-                    rhs_scale=x_scales[a][:, h * HALF : (h + 1) * HALF],
+                    rhs=x_codes[a][:, i * n : (i + 1) * n].bitcast(FP8X4),
+                    rhs_scale=x_scales[a][:, i * n : (i + 1) * n],
                     start=(a == 0),
                     stop=(a == PASSES - 1),
                 )
 
         def empty(m):
+            y[m] = keep.tile([P, S], F32, name=f"y{m}", tag=f"slot{(m + 1) % BLOCKS}_{Y_SLOT[m]}")
             for h in range(HALVES):
-                nc.scalar.copy(out=y[m][h][:], in_=acc[m][h][:])
+                source = acc[m][h][:] if len(acc[m]) > 1 else acc[m][0][:, h * HALF : (h + 1) * HALF]
+                nc.scalar.copy(out=y[m][:, h * HALF : (h + 1) * HALF], in_=source)
 
         def scatter(m, h):
             nc.vector.tensor_tensor(
                 windows[m][:].indirect(offsets[:, h * LIST_COLS : (h + 1) * LIST_COLS]),
-                y[m][h][:],
+                y[m][:, h * HALF : (h + 1) * HALF],
                 weights[:, h * HALF : (h + 1) * HALF],
                 MULT,
             )
@@ -91,12 +95,17 @@ def tile_list_hscat_none_kernel(tc, x, w, wgo, offs, out):
         def store(m):
             nc.sync.dma_start(out=out[m * P : (m + 1) * P, :], in_=windows[m][:])
 
+        def group_w(copy, m, a, c0=0, c1=P):
+            interleave(copy, w_grouped[m], w_raw[m][a], c0, c1, base=a * P)
+
         for a in range(PASSES):
             load_x(a)
             load_w(0, a)
+        for a in range(PASSES):
+            load_w(1, a)
         nc.sync.dma_start(offsets[:], offs)
         nc.sync.dma_start(out=weights[:], in_=wgo)
-        for m in range(1, BLOCKS):
+        for m in range(2, BLOCKS):
             for a in range(PASSES):
                 load_w(m, a)
 
@@ -106,24 +115,24 @@ def tile_list_hscat_none_kernel(tc, x, w, wgo, offs, out):
         for a in range(PASSES):
             interleave(nc.scalar.copy, x_grouped[a], x_raw[a], 0, X_SPLIT)
             interleave(nc.vector.tensor_copy, x_grouped[a], x_raw[a], X_SPLIT, S)
+            group_w(nc.scalar.copy, 0, a, 0, W_SPLIT)
+            group_w(nc.vector.tensor_copy, 0, a, W_SPLIT, P)
             quantise(x_codes[a], x_scales[a], x_grouped[a], 0, S)
-            interleave(nc.scalar.copy, w_grouped[0], w_raw[0][a], 0, W_SPLIT, base=a * P)
-            interleave(nc.vector.tensor_copy, w_grouped[0], w_raw[0][a], W_SPLIT, P, base=a * P)
             quantise(w_codes[0], w_scales[0], w_grouped[0], a * P, (a + 1) * P)
             multiply(0, a)
+        group_w(nc.vector.tensor_copy, 1, 0)
+        group_w(nc.scalar.copy, 1, 1, 0, W_SPLIT)
+        group_w(nc.vector.tensor_copy, 1, 1, W_SPLIT, P)
         empty(0)
-        interleave(nc.vector.tensor_copy, w_grouped[1], w_raw[1][0], 0, P)
-        interleave(nc.scalar.copy, w_grouped[1], w_raw[1][1], 0, P, base=P)
-
+        for m in range(1, BLOCKS):
+            if m > 1:
+                for a in range(PASSES):
+                    group_w(nc.scalar.copy, m, a)
+            quantise(w_codes[m], w_scales[m], w_grouped[m], 0, PASSES * P)
+            for a in range(PASSES):
+                multiply(m, a)
+            empty(m)
         for m in range(BLOCKS):
-            scatter(m, 0)
-            if m + 1 < BLOCKS:
-                quantise(w_codes[m + 1], w_scales[m + 1], w_grouped[m + 1], 0, PASSES * P)
-                for a in range(PASSES):
-                    multiply(m + 1, a)
-                empty(m + 1)
-            if m + 2 < BLOCKS:
-                for a in range(PASSES):
-                    interleave(nc.scalar.copy, w_grouped[m + 2], w_raw[m + 2][a], 0, P, base=a * P)
-            scatter(m, 1)
+            for h in range(HALVES):
+                scatter(m, h)
             store(m)

@@ -21,9 +21,9 @@ BLOCKS = M // P
 HALF = S // 2
 HALVES = S // HALF
 LIST_COLS = HALF // 16
+RUN = 4
 X_SPLIT = 96
 W_SPLIT = 64
-Y_SLOT = (1, 0, 0, 0)
 
 
 def tile_list_hscat_none_kernel(tc, x, w, wgo, offs, out):
@@ -39,11 +39,11 @@ def tile_list_hscat_none_kernel(tc, x, w, wgo, offs, out):
         x_grouped = [keep.tile([P, S, PACK], BF16, name=f"x_grouped{a}", align_bytes=64) for a in range(PASSES)]
         x_codes = [keep.tile([P, S], U32, name=f"x_codes{a}", align_bytes=64) for a in range(PASSES)]
         x_scales = [keep.tile([P, S], U8, name=f"x_scales{a}", align_bytes=64) for a in range(PASSES)]
-        w_grouped = [keep.tile([P, PASSES * P, PACK], BF16, name=f"w_grouped{m}", align_bytes=64) for m in range(BLOCKS)]
-        w_codes = [keep.tile([P, PASSES * P], U32, name=f"w_codes{m}", align_bytes=64) for m in range(BLOCKS)]
-        w_scales = [keep.tile([P, PASSES * P], U8, name=f"w_scales{m}", align_bytes=64) for m in range(BLOCKS)]
+        w_grouped = [[keep.tile([P, P, PACK], BF16, name=f"w_grouped{m}_{a}", align_bytes=64) for a in range(PASSES)] for m in range(BLOCKS)]
+        w_codes = [[keep.tile([P, P], U32, name=f"w_codes{m}_{a}", align_bytes=64) for a in range(PASSES)] for m in range(BLOCKS)]
+        w_scales = [[keep.tile([P, P], U8, name=f"w_scales{m}_{a}", align_bytes=64) for a in range(PASSES)] for m in range(BLOCKS)]
         windows = [keep.tile([P, T], F32, name=f"window{m}") for m in range(BLOCKS)]
-        acc = [[psum.tile([P, HALF], F32, name=f"acc{m}_{h}") for h in range(HALVES)] for m in range(1)] + [[psum.tile([P, S], F32, name=f"acc{m}")] for m in range(1, BLOCKS)]
+        acc = [[psum.tile([P, HALF], F32, name=f"acc{m}_{h}") for h in range(HALVES)] for m in range(BLOCKS)]
         y = {}
 
         def load_x(a):
@@ -55,48 +55,51 @@ def tile_list_hscat_none_kernel(tc, x, w, wgo, offs, out):
                 in_=w[a * K_PASS : (a + 1) * K_PASS, m * P : (m + 1) * P].rearrange("(p j) n -> p j n", j=PACK),
             )
 
-        def interleave(copy, grouped, raw, c0, c1, base=0):
-            copy(out=grouped[:, base + c0 : base + c1, :], in_=raw[:, :, c0:c1].rearrange("p j c -> p c j"))
-
-        def quantise(codes, scales, grouped, c0, c1):
-            nc.vector.quantize_mx(
-                out=codes[:, c0:c1].bitcast(FP8X4),
-                scales=scales[:, c0:c1],
-                in_=grouped[:, c0:c1, :].rearrange("p c j -> p (c j)"),
+        def interleave(copy, grouped, raw, c0, c1):
+            copy(
+                out=grouped[:, c0:c1, :].rearrange("p (c i) j -> p c j i", i=RUN),
+                in_=raw[:, :, c0:c1].rearrange("p j (c i) -> p c j i", i=RUN),
             )
 
+        def group_w(copy, m, a, c0=0, c1=P):
+            interleave(copy, w_grouped[m][a], w_raw[m][a], c0, c1)
+
+        def quantise(codes, scales, grouped):
+            nc.vector.quantize_mx(
+                out=codes[:].bitcast(FP8X4),
+                scales=scales[:],
+                in_=grouped[:].rearrange("p c j -> p (c j)"),
+            )
+
+        def quantise_w(m, a):
+            quantise(w_codes[m][a], w_scales[m][a], w_grouped[m][a])
+
         def multiply(m, a):
-            for i, bank in enumerate(acc[m]):
-                n = S // len(acc[m])
+            for h in range(HALVES):
                 nc.tensor.matmul_mx(
-                    out=bank[:],
-                    lhsT=w_codes[m][:, a * P : (a + 1) * P].bitcast(FP8X4),
-                    lhsT_scale=w_scales[m][:, a * P : (a + 1) * P],
-                    rhs=x_codes[a][:, i * n : (i + 1) * n].bitcast(FP8X4),
-                    rhs_scale=x_scales[a][:, i * n : (i + 1) * n],
+                    out=acc[m][h][:],
+                    lhsT=w_codes[m][a][:].bitcast(FP8X4),
+                    lhsT_scale=w_scales[m][a][:],
+                    rhs=x_codes[a][:, h * HALF : (h + 1) * HALF].bitcast(FP8X4),
+                    rhs_scale=x_scales[a][:, h * HALF : (h + 1) * HALF],
                     start=(a == 0),
                     stop=(a == PASSES - 1),
                 )
 
-        def empty(m):
-            y[m] = keep.tile([P, S], F32, name=f"y{m}", tag=f"slot{(m + 1) % BLOCKS}_{Y_SLOT[m]}")
-            for h in range(HALVES):
-                source = acc[m][h][:] if len(acc[m]) > 1 else acc[m][0][:, h * HALF : (h + 1) * HALF]
-                nc.scalar.copy(out=y[m][:, h * HALF : (h + 1) * HALF], in_=source)
+        def empty(m, h):
+            y[m, h] = keep.tile([P, HALF], F32, name=f"y{m}_{h}", tag=f"slot{(m + 1) % BLOCKS}_{h}")
+            nc.scalar.copy(out=y[m, h][:], in_=acc[m][h][:])
 
         def scatter(m, h):
             nc.vector.tensor_tensor(
                 windows[m][:].indirect(offsets[:, h * LIST_COLS : (h + 1) * LIST_COLS]),
-                y[m][:, h * HALF : (h + 1) * HALF],
+                y[m, h][:],
                 weights[:, h * HALF : (h + 1) * HALF],
                 MULT,
             )
 
         def store(m):
             nc.sync.dma_start(out=out[m * P : (m + 1) * P, :], in_=windows[m][:])
-
-        def group_w(copy, m, a, c0=0, c1=P):
-            interleave(copy, w_grouped[m], w_raw[m][a], c0, c1, base=a * P)
 
         for a in range(PASSES):
             load_x(a)
@@ -117,21 +120,21 @@ def tile_list_hscat_none_kernel(tc, x, w, wgo, offs, out):
             interleave(nc.vector.tensor_copy, x_grouped[a], x_raw[a], X_SPLIT, S)
             group_w(nc.scalar.copy, 0, a, 0, W_SPLIT)
             group_w(nc.vector.tensor_copy, 0, a, W_SPLIT, P)
-            quantise(x_codes[a], x_scales[a], x_grouped[a], 0, S)
-            quantise(w_codes[0], w_scales[0], w_grouped[0], a * P, (a + 1) * P)
+            quantise(x_codes[a], x_scales[a], x_grouped[a])
+            quantise_w(0, a)
             multiply(0, a)
         group_w(nc.vector.tensor_copy, 1, 0)
         group_w(nc.scalar.copy, 1, 1, 0, W_SPLIT)
         group_w(nc.vector.tensor_copy, 1, 1, W_SPLIT, P)
-        empty(0)
         for m in range(1, BLOCKS):
-            if m > 1:
-                for a in range(PASSES):
-                    group_w(nc.scalar.copy, m, a)
-            quantise(w_codes[m], w_scales[m], w_grouped[m], 0, PASSES * P)
             for a in range(PASSES):
+                if m > 1:
+                    group_w(nc.scalar.copy, m, a)
+                empty(m - 1, a)
+                quantise_w(m, a)
                 multiply(m, a)
-            empty(m)
+        for h in range(HALVES):
+            empty(BLOCKS - 1, h)
         for m in range(BLOCKS):
             for h in range(HALVES):
                 scatter(m, h)

from contextlib import ExitStack

import concourse.mybir as mybir

K, M, T, S = 1024, 512, 512, 256
FLOPS = 2 * K * M * S

F32 = mybir.dt.float32
BF16 = mybir.dt.bfloat16
U32 = mybir.dt.uint32
U16 = mybir.dt.uint16
U8 = mybir.dt.uint8
FP8X4 = mybir.dt.float8_e4m3fn_x4
MULT = mybir.AluOpType.mult

P = 128
PACK = 4
K_PASS = P * PACK
PASSES = K // K_PASS
BLOCKS = M // P
HALF = S // 2
HALVES = S // HALF
LIST_COLS = HALF // 16
RUN = 4
X_SPLIT = 96
W_SPLIT = 64


def tile_list_hscat_none_kernel(tc, x, w, wgo, offs, out):
    nc = tc.nc
    with ExitStack() as ctx:
        keep = ctx.enter_context(tc.tile_pool(name="keep", bufs=1))
        psum = ctx.enter_context(tc.psum_pool(name="psum", bufs=1))

        offsets = keep.tile([P, S // 16], U16, name="offsets")
        weights = keep.tile([P, S], F32, name="weights")
        x_raw = [keep.tile([P, PACK, S], F32, name=f"x_raw{a}") for a in range(PASSES)]
        w_raw = [[keep.tile([P, PACK, P], F32, name=f"w_raw{m}_{a}", tag=f"slot{m}_{a}") for a in range(PASSES)] for m in range(BLOCKS)]
        x_grouped = [keep.tile([P, S, PACK], BF16, name=f"x_grouped{a}", align_bytes=64) for a in range(PASSES)]
        x_codes = [keep.tile([P, S], U32, name=f"x_codes{a}", align_bytes=64) for a in range(PASSES)]
        x_scales = [keep.tile([P, S], U8, name=f"x_scales{a}", align_bytes=64) for a in range(PASSES)]
        w_grouped = [[keep.tile([P, P, PACK], BF16, name=f"w_grouped{m}_{a}", align_bytes=64) for a in range(PASSES)] for m in range(BLOCKS)]
        w_codes = [[keep.tile([P, P], U32, name=f"w_codes{m}_{a}", align_bytes=64) for a in range(PASSES)] for m in range(BLOCKS)]
        w_scales = [[keep.tile([P, P], U8, name=f"w_scales{m}_{a}", align_bytes=64) for a in range(PASSES)] for m in range(BLOCKS)]
        windows = [keep.tile([P, T], F32, name=f"window{m}") for m in range(BLOCKS)]
        acc = [[psum.tile([P, HALF], F32, name=f"acc{m}_{h}") for h in range(HALVES)] for m in range(BLOCKS)]
        y = {}

        def load_x(a):
            nc.sync.dma_start(out=x_raw[a][:], in_=x[a * K_PASS : (a + 1) * K_PASS, :].rearrange("(p j) s -> p j s", j=PACK))

        def load_w(m, a):
            nc.sync.dma_start(
                out=w_raw[m][a][:],
                in_=w[a * K_PASS : (a + 1) * K_PASS, m * P : (m + 1) * P].rearrange("(p j) n -> p j n", j=PACK),
            )

        def interleave(copy, grouped, raw, c0, c1):
            copy(
                out=grouped[:, c0:c1, :].rearrange("p (c i) j -> p c j i", i=RUN),
                in_=raw[:, :, c0:c1].rearrange("p j (c i) -> p c j i", i=RUN),
            )

        def group_w(copy, m, a, c0=0, c1=P):
            interleave(copy, w_grouped[m][a], w_raw[m][a], c0, c1)

        def quantise(codes, scales, grouped):
            nc.vector.quantize_mx(
                out=codes[:].bitcast(FP8X4),
                scales=scales[:],
                in_=grouped[:].rearrange("p c j -> p (c j)"),
            )

        def quantise_w(m, a):
            quantise(w_codes[m][a], w_scales[m][a], w_grouped[m][a])

        def multiply(m, a):
            for h in range(HALVES):
                nc.tensor.matmul_mx(
                    out=acc[m][h][:],
                    lhsT=w_codes[m][a][:].bitcast(FP8X4),
                    lhsT_scale=w_scales[m][a][:],
                    rhs=x_codes[a][:, h * HALF : (h + 1) * HALF].bitcast(FP8X4),
                    rhs_scale=x_scales[a][:, h * HALF : (h + 1) * HALF],
                    start=(a == 0),
                    stop=(a == PASSES - 1),
                )

        def empty(m, h):
            y[m, h] = keep.tile([P, HALF], F32, name=f"y{m}_{h}", tag=f"slot{(m + 1) % BLOCKS}_{h}")
            nc.scalar.copy(out=y[m, h][:], in_=acc[m][h][:])

        def scatter(m, h):
            nc.vector.tensor_tensor(
                windows[m][:].indirect(offsets[:, h * LIST_COLS : (h + 1) * LIST_COLS]),
                y[m, h][:],
                weights[:, h * HALF : (h + 1) * HALF],
                MULT,
            )

        def store(m):
            nc.sync.dma_start(out=out[m * P : (m + 1) * P, :], in_=windows[m][:])

        for a in range(PASSES):
            load_x(a)
            load_w(0, a)
        for a in range(PASSES):
            load_w(1, a)
        nc.sync.dma_start(offsets[:], offs)
        nc.sync.dma_start(out=weights[:], in_=wgo)
        for m in range(2, BLOCKS):
            for a in range(PASSES):
                load_w(m, a)

        for m in range(BLOCKS):
            nc.gpsimd.memset(windows[m][:], 0.0)

        for a in range(PASSES):
            interleave(nc.scalar.copy, x_grouped[a], x_raw[a], 0, X_SPLIT)
            interleave(nc.vector.tensor_copy, x_grouped[a], x_raw[a], X_SPLIT, S)
            group_w(nc.scalar.copy, 0, a, 0, W_SPLIT)
            group_w(nc.vector.tensor_copy, 0, a, W_SPLIT, P)
            quantise(x_codes[a], x_scales[a], x_grouped[a])
            quantise_w(0, a)
            multiply(0, a)
        group_w(nc.vector.tensor_copy, 1, 0)
        group_w(nc.scalar.copy, 1, 1, 0, W_SPLIT)
        group_w(nc.vector.tensor_copy, 1, 1, W_SPLIT, P)
        for m in range(1, BLOCKS):
            for a in range(PASSES):
                if m > 1:
                    group_w(nc.scalar.copy, m, a)
                empty(m - 1, a)
                quantise_w(m, a)
                multiply(m, a)
        for h in range(HALVES):
            empty(BLOCKS - 1, h)
        for m in range(BLOCKS):
            for h in range(HALVES):
                scatter(m, h)
            store(m)
